import numpy as np, ml_dtypes
CORES = [8,80,112,136,208,240,264,336,368,392,464,496]
N = 12
KB, QP, ROOT = 1, 64, 0
def setup_inputs(rng):
    return {"q": rng.standard_normal((N, 128, QP), dtype=np.float32).astype(ml_dtypes.bfloat16), "k": rng.standard_normal((N, 128, KB * 128), dtype=np.float32).astype(ml_dtypes.bfloat16), "v": rng.standard_normal((N, 128, KB * 128), dtype=np.float32).astype(ml_dtypes.bfloat16)}
def setup_inputs_big(rng):
    d = setup_inputs(rng)
    for k in ("q", "k", "v"): d[k] = (d[k].astype(np.float32) * 1024.0).astype(d[k].dtype)
    return d
def setup_inputs_small(rng):
    d = setup_inputs(rng)
    for k in ("q", "k", "v"): d[k] = (d[k].astype(np.float32) * (1 / 1024.0)).astype(d[k].dtype)
    return d
def setup_inputs_apart(rng):
    d = setup_inputs(rng)
    f = (10.0 ** rng.permutation(np.linspace(-1.5, 1.5, N))).astype(np.float32).reshape(N, 1, 1)
    for k in ("q", "k", "v"): d[k] = (d[k].astype(np.float32) * f).astype(d[k].dtype)
    return d
def reference(q, k, v):
    Q, K, V = q.astype(np.float64), k.astype(np.float64), v.astype(np.float64)
    o = np.zeros((128, QP))
    for j in range(N):
        for b in range(KB):
            o += V[j][:, 128 * b:128 * b + 128].T @ np.maximum(K[j][:, 128 * b:128 * b + 128].T @ Q[ROOT], 0.0)
    y = np.full((N, 128, QP), np.nan)
    y[ROOT] = o
    return {"y": y.astype(ml_dtypes.bfloat16 if q.dtype != np.float64 else np.float64)}

@@ -1,0 +1,197 @@
+from concourse.bass import DstId, RemoteDMATransfer
+from concourse.mybir import AluOpType
+
+N = 12
+KP = 128
+QP = 64
+NB = 4
+HOSTS = 4
+
+SCRATCH = {
+    "kv": ("sbuf", [128, N * 2 * KP], "bfloat16"),
+    "qs": ("sbuf", [128, QP], "bfloat16"),
+    "sb": ("sbuf", [128, N * QP], "bfloat16"),
+    "zero": ("sbuf", [128, QP], "float32"),
+    "ysb": ("sbuf", [128, QP], "bfloat16"),
+    "st": ("dram", [2, 128, KP], "bfloat16"),
+    "rl": ("dram", [128, KP], "bfloat16"),
+    "ps0": ("psum", [128, 512], "float32"),
+    "ps1": ("psum", [128, 512], "float32"),
+    "ps2": ("psum", [128, 512], "float32"),
+    "ps3": ("psum", [128, 512], "float32"),
+    "po": ("psum", [128, 512], "float32"),
+}
+SEMAPHORES = (["ld", "sent", "inn", "zs", "so", "sy", "st"]
+              + ["s%d" % b for b in range(NB)] + ["r%d" % b for b in range(NB)]
+              + ["k%d" % j for j in range(1, N)] + ["v%d" % j for j in range(1, N)])
+
+_CACHE = {}
+
+
+def _bits(m):
+    return [1 << i for i in range(16) if (m >> i) & 1]
+
+
+def _plan(T, topo):
+    if "plan" in _CACHE:
+        return _CACHE["plan"]
+    cores = list(T.cores)
+    root = cores[T.root]
+    by_chip = {}
+    for c in range(HOSTS * topo.CORES_PER_HOST):
+        by_chip.setdefault((topo.host(c), topo.chip(c)), []).append(c)
+
+    def key(c):
+        return (topo.host(c), topo.chip(c))
+
+    def mate_key(c):
+        for kk, cs in by_chip.items():
+            if topo.mates(c, cs[0]):
+                return kk
+
+    def owners(kk):
+        other = by_chip[mate_key(by_chip[kk][0])][0]
+        return [x for x in by_chip[kk] if topo.may_write(x, other)]
+
+    used = set(cores)
+
+    def take(pool, d):
+        for x in pool:
+            if x not in used and topo.die(x) == d:
+                used.add(x)
+                return x
+
+    direct, relay = [], {}
+    for j, s in enumerate(cores):
+        if s == root:
+            continue
+        if topo.may_write(s, root):
+            direct.append(j)
+            continue
+        same_rack = topo.rack(topo.host(s)) == topo.rack(topo.host(root))
+        if [x for x in owners(key(s)) if topo.may_write(x, root)]:
+            if same_rack and topo.host(s) != topo.host(root):
+                pool = owners(mate_key(root))
+            else:
+                pool = owners(key(s))
+        elif topo.chip(s) == topo.chip(root):
+            kk = [k2 for k2 in by_chip if k2[1] == topo.chip(root) and k2[0] != topo.host(s)
+                  and topo.rack(k2[0]) == topo.rack(topo.host(s))][0]
+            own = owners(kk)
+            pool = [x for x in by_chip[kk] if x not in own]
+        else:
+            kk = [k2 for k2 in by_chip if k2[1] == topo.chip(s) and topo.rack(k2[0]) == topo.rack(topo.host(root))
+                  and topo.may_write(s, by_chip[k2][0])][0]
+            pool = owners(kk)
+        dies = [topo.die(s)] + [d for d in (0, 1) if d != topo.die(s)]
+        for piece in (0, 1):
+            relay[(j, piece)] = take(pool, dies[piece])
+    _CACHE["plan"] = (direct, relay)
+    return _CACHE["plan"]
+
+
+def _root_program(g, core, T, topo, direct, relay):
+    sem = T.sem
+    g.sync.dma_start(T.qs[:], T.q[:]).then_inc(sem.ld, 16)
+    g.scalar.dma_start(T.kv[:, 0:KP], T.k[:]).then_inc(sem.ld, 16)
+    g.sync.dma_start(T.kv[:, KP:2 * KP], T.v[:]).then_inc(sem.ld, 16)
+    g.vector.memset(T.zero[:], 0.0).then_inc(sem.zs, 1)
+    g.vector.wait_ge(sem.zs, 1)
+    g.tensor.wait_ge(sem.ld, 48)
+
+    cores = list(T.cores)
+
+    def hops(j):
+        if j == T.root:
+            return 0
+        if j in direct:
+            return 1
+        x = relay[(j, 0)]
+        on_chip = (topo.host(x), topo.chip(x)) == (topo.host(cores[j]), topo.chip(cores[j]))
+        return 2 if on_chip else 3
+
+    order = sorted(range(N), key=lambda j: (hops(j), j))
+    ps = [T["ps%d" % b] for b in range(NB)]
+
+    def landed(j, piece):
+        if j == T.root or (piece == 1 and j in direct):
+            return
+        src = cores[j] if j in direct else relay[(j, piece)]
+        g.tensor.wait_ge(sem["%s%d" % ("kv"[piece], j)], len(_bits(topo.mask(src, core))))
+
+    def second(i):
+        j = order[i]
+        g.tensor.wait_ge(sem["r%d" % (i % NB)], i // NB + 1)
+        landed(j, 1)
+        mm = g.tensor.matmul(T.po[:, 0:QP], T.kv[:, (2 * j + 1) * KP:(2 * j + 2) * KP], T.sb[:, i * QP:(i + 1) * QP],
+                             start=(i == 0), stop=(i == N - 1))
+        if i == N - 1:
+            mm.then_inc(sem.so, 1)
+
+    for i, j in enumerate(order):
+        b = i % NB
+        landed(j, 0)
+        g.tensor.matmul(ps[b][:, 0:QP], T.kv[:, 2 * j * KP:(2 * j + 1) * KP], T.qs[:],
+                        start=True, stop=True).then_inc(sem["s%d" % b], 1)
+        g.vector.wait_ge(sem["s%d" % b], i // NB + 1)
+        g.vector.tensor_tensor(T.sb[:, i * QP:(i + 1) * QP], ps[b][:, 0:QP], T.zero[:],
+                               op=AluOpType.max).then_inc(sem["r%d" % b], 1)
+        if i >= 1:
+            second(i - 1)
+    second(N - 1)
+    g.vector.wait_ge(sem.so, 1)
+    g.vector.tensor_copy(T.ysb[:], T.po[:, 0:QP]).then_inc(sem.sy, 1)
+    g.sync.wait_ge(sem.sy, 1)
+    g.sync.dma_start(T.y[:], T.ysb[:]).then_inc(sem.st, 16)
+    g.sync.wait_ge(sem.st, 16)
+
+
+def rank_program(g, core, T, topo):
+    direct, relay = _plan(T, topo)
+    cores = list(T.cores)
+    root = cores[T.root]
+    sem = T.sem
+    rank = T.rank_of(core)
+
+    if core == root:
+        _root_program(g, core, T, topo, direct, relay)
+        return
+
+    if rank is not None and rank in direct:
+        g.sync.dma_start(T.kv[:, 0:KP], T.k[:]).then_inc(sem.ld, 16)
+        g.scalar.dma_start(T.kv[:, KP:2 * KP], T.v[:]).then_inc(sem.ld, 16)
+        g.wait_ge(sem.ld, 32)
+        rid, pid = topo.addr(root, core)
+        m = topo.mask(core, root)
+        g.remote_dma(T.kv[:, 2 * rank * KP:(2 * rank + 2) * KP], T.kv[:, 0:2 * KP], sem["k%d" % rank], sem.sent,
+                     pid, rid, m)
+        g.wait_ge(sem.sent, len(_bits(m)))
+        return
+
+    if rank is not None:
+        g.sync.dma_start(T.st[0], T.k[:]).then_inc(sem.ld, 16)
+        g.scalar.dma_start(T.st[1], T.v[:]).then_inc(sem.ld, 16)
+        g.wait_ge(sem.ld, 32)
+        xs = [relay[(rank, 0)], relay[(rank, 1)]]
+        eng = _bits(topo.mask(core, xs[0]) & topo.mask(core, xs[1]))
+        half = len(eng) // 2
+        step = half // 4
+        masks = [sum(eng[half::step]), sum(eng[0:half:step])]
+        tr = []
+        for piece in (0, 1):
+            rid, pid = topo.addr(xs[piece], core)
+            tr.append(RemoteDMATransfer(dst_ids=[DstId(rid=rid, pnc=pid)], dma_engine_mask=masks[piece],
+                                        remote_sem=sem.inn, src=T.st[piece], dst=T.rl[:]))
+        g.remote_dma_fused(tr, local_sem=sem.sent)
+        g.wait_ge(sem.sent, len(_bits(masks[0])) + len(_bits(masks[1])))
+        return
+
+    for (j, piece), x in relay.items():
+        if x != core:
+            continue
+        g.wait_ge(sem.inn, 4)
+        rid, pid = topo.addr(root, core)
+        m = topo.mask(core, root)
+        a = (2 * j + piece) * KP
+        g.remote_dma(T.kv[:, a:a + KP], T.rl[:], sem["%s%d" % ("kv"[piece], j)], sem.sent, pid, rid, m)
+        g.wait_ge(sem.sent, len(_bits(m)))

@@ -4,25 +4,25 @@ from concourse.mybir import AluOpType
 N = 12
 KP = 128
 QP = 64
-NB = 4
+NG = 7
 HOSTS = 4
+E1 = 4
+E2 = 8
 
 SCRATCH = {
     "kv": ("sbuf", [128, N * 2 * KP], "bfloat16"),
     "qs": ("sbuf", [128, QP], "bfloat16"),
     "sb": ("sbuf", [128, N * QP], "bfloat16"),
-    "zero": ("sbuf", [128, QP], "float32"),
+    "zero": ("sbuf", [128, 2 * QP], "float32"),
     "ysb": ("sbuf", [128, QP], "bfloat16"),
     "st": ("dram", [2, 128, KP], "bfloat16"),
-    "rl": ("dram", [128, KP], "bfloat16"),
-    "ps0": ("psum", [128, 512], "float32"),
-    "ps1": ("psum", [128, 512], "float32"),
-    "ps2": ("psum", [128, 512], "float32"),
-    "ps3": ("psum", [128, 512], "float32"),
+    "rl": ("dram", [2, 128, KP], "bfloat16"),
     "po": ("psum", [128, 512], "float32"),
 }
-SEMAPHORES = (["ld", "sent", "inn", "zs", "so", "sy", "st"]
-              + ["s%d" % b for b in range(NB)] + ["r%d" % b for b in range(NB)]
+for _b in range(NG):
+    SCRATCH["ps%d" % _b] = ("psum", [128, 512], "float32")
+SEMAPHORES = (["ld", "sent", "inn0", "inn1", "zs", "so", "sy", "st"]
+              + ["s%d" % b for b in range(NG)] + ["r%d" % b for b in range(NG)]
               + ["k%d" % j for j in range(1, N)] + ["v%d" % j for j in range(1, N)])
 
 _CACHE = {}
@@ -30,6 +30,10 @@ _CACHE = {}
 
 def _bits(m):
     return [1 << i for i in range(16) if (m >> i) & 1]
+
+
+def _spread(eng, n):
+    return sum(eng[::len(eng) // n])
 
 
 def _plan(T, topo):
@@ -53,39 +57,47 @@ def _plan(T, topo):
         other = by_chip[mate_key(by_chip[kk][0])][0]
         return [x for x in by_chip[kk] if topo.may_write(x, other)]
 
-    used = set(cores)
+    load = {}
 
-    def take(pool, d):
-        for x in pool:
-            if x not in used and topo.die(x) == d:
-                used.add(x)
-                return x
+    def give(x):
+        load[x] = load.get(x, 0) + 1
+        return (x, load[x] - 1)
 
-    direct, relay = [], {}
+    def fresh(pool, d):
+        return give([x for x in pool if x not in cores and x not in load and topo.die(x) == d][0])
+
+    def again(pool, d):
+        return give([x for x in pool if load.get(x, 0) == 1 and topo.die(x) == d][0])
+
+    direct = [j for j, s in enumerate(cores) if s != root and topo.may_write(s, root)]
+    relay = {}
+    over_mate = set()
     for j, s in enumerate(cores):
-        if s == root:
+        if s == root or j in direct:
             continue
-        if topo.may_write(s, root):
-            direct.append(j)
-            continue
-        same_rack = topo.rack(topo.host(s)) == topo.rack(topo.host(root))
+        my_rack = topo.rack(topo.host(s))
+        root_rack = topo.rack(topo.host(root))
+        d_own = topo.die(s)
+        d_other = [d for d in (0, 1) if d != d_own][0]
         if [x for x in owners(key(s)) if topo.may_write(x, root)]:
-            if same_rack and topo.host(s) != topo.host(root):
-                pool = owners(mate_key(root))
-            else:
-                pool = owners(key(s))
+            kk = key(s)
+            if my_rack not in over_mate:
+                over_mate.add(my_rack)
+                kk = (topo.host(root) if my_rack == root_rack else topo.host(s), mate_key(root)[1])
+            relay[(j, 0)] = fresh(owners(kk), d_own)
+            relay[(j, 1)] = fresh(owners(kk), d_other)
         elif topo.chip(s) == topo.chip(root):
-            kk = [k2 for k2 in by_chip if k2[1] == topo.chip(root) and k2[0] != topo.host(s)
-                  and topo.rack(k2[0]) == topo.rack(topo.host(s))][0]
-            own = owners(kk)
-            pool = [x for x in by_chip[kk] if x not in own]
+            via = [cores[d] for d in direct if topo.may_write(s, cores[d])]
+            near = [x for x in via if topo.rack(topo.host(x)) == my_rack][0]
+            far = [x for x in via if topo.rack(topo.host(x)) != my_rack][0]
+            own = owners(key(near))
+            relay[(j, 0)] = fresh([x for x in by_chip[key(near)] if x not in own], d_other)
+            relay[(j, 1)] = give(far)
         else:
-            kk = [k2 for k2 in by_chip if k2[1] == topo.chip(s) and topo.rack(k2[0]) == topo.rack(topo.host(root))
+            kk = [k2 for k2 in by_chip if k2[1] == topo.chip(s) and topo.rack(k2[0]) == root_rack
                   and topo.may_write(s, by_chip[k2][0])][0]
-            pool = owners(kk)
-        dies = [topo.die(s)] + [d for d in (0, 1) if d != topo.die(s)]
-        for piece in (0, 1):
-            relay[(j, piece)] = take(pool, dies[piece])
+            relay[(j, 0)] = again(owners(kk), d_own)
+            relay[(j, 1)] = again(owners(kk), d_other)
     _CACHE["plan"] = (direct, relay)
     return _CACHE["plan"]
 
@@ -106,39 +118,56 @@ def _root_program(g, core, T, topo, direct, relay):
             return 0
         if j in direct:
             return 1
-        x = relay[(j, 0)]
+        x = relay[(j, 0)][0]
         on_chip = (topo.host(x), topo.chip(x)) == (topo.host(cores[j]), topo.chip(cores[j]))
         return 2 if on_chip else 3
 
-    order = sorted(range(N), key=lambda j: (hops(j), j))
-    ps = [T["ps%d" % b] for b in range(NB)]
+    groups = []
+    place = 0
+    for cl in range(4):
+        js = [j for j in range(N) if hops(j) == cl]
+        js.sort(key=lambda j: (relay[(j, 0)][1] if (j, 0) in relay else 0, j))
+        for a in range(0, len(js), 2):
+            groups.append((cl, js[a:a + 2], place))
+            place += len(js[a:a + 2])
+    total = [0]
 
     def landed(j, piece):
         if j == T.root or (piece == 1 and j in direct):
             return
-        src = cores[j] if j in direct else relay[(j, piece)]
-        g.tensor.wait_ge(sem["%s%d" % ("kv"[piece], j)], len(_bits(topo.mask(src, core))))
+        n = len(_bits(topo.mask(cores[j], core))) if j in direct else E2
+        g.tensor.wait_ge(sem["%s%d" % ("kv"[piece], j)], n)
 
-    def second(i):
-        j = order[i]
-        g.tensor.wait_ge(sem["r%d" % (i % NB)], i // NB + 1)
-        landed(j, 1)
-        mm = g.tensor.matmul(T.po[:, 0:QP], T.kv[:, (2 * j + 1) * KP:(2 * j + 2) * KP], T.sb[:, i * QP:(i + 1) * QP],
-                             start=(i == 0), stop=(i == N - 1))
-        if i == N - 1:
-            mm.then_inc(sem.so, 1)
+    def first(gi):
+        _, js, at = groups[gi]
+        ps = T["ps%d" % gi]
+        for t, j in enumerate(js):
+            landed(j, 0)
+            g.tensor.matmul(ps[:, t * QP:(t + 1) * QP], T.kv[:, 2 * j * KP:(2 * j + 1) * KP], T.qs[:],
+                            start=True, stop=True).then_inc(sem["s%d" % gi], 1)
+        w = len(js) * QP
+        g.vector.wait_ge(sem["s%d" % gi], len(js))
+        g.vector.tensor_tensor(T.sb[:, at * QP:at * QP + w], ps[:, 0:w], T.zero[:, 0:w],
+                               op=AluOpType.max).then_inc(sem["r%d" % gi], 1)
 
-    for i, j in enumerate(order):
-        b = i % NB
-        landed(j, 0)
-        g.tensor.matmul(ps[b][:, 0:QP], T.kv[:, 2 * j * KP:(2 * j + 1) * KP], T.qs[:],
-                        start=True, stop=True).then_inc(sem["s%d" % b], 1)
-        g.vector.wait_ge(sem["s%d" % b], i // NB + 1)
-        g.vector.tensor_tensor(T.sb[:, i * QP:(i + 1) * QP], ps[b][:, 0:QP], T.zero[:],
-                               op=AluOpType.max).then_inc(sem["r%d" % b], 1)
-        if i >= 1:
-            second(i - 1)
-    second(N - 1)
+    def second(gi):
+        _, js, at = groups[gi]
+        g.tensor.wait_ge(sem["r%d" % gi], 1)
+        for t, j in enumerate(js):
+            landed(j, 1)
+            total[0] += 1
+            mm = g.tensor.matmul(T.po[:, 0:QP], T.kv[:, (2 * j + 1) * KP:(2 * j + 2) * KP],
+                                 T.sb[:, (at + t) * QP:(at + t + 1) * QP], start=(total[0] == 1), stop=(total[0] == N))
+            if total[0] == N:
+                mm.then_inc(sem.so, 1)
+
+    early = [gi for gi in range(len(groups)) if groups[gi][0] <= 1]
+    late = [gi for gi in range(len(groups)) if groups[gi][0] > 1]
+    for part in (early, late):
+        for gi in part:
+            first(gi)
+        for gi in part:
+            second(gi)
     g.vector.wait_ge(sem.so, 1)
     g.vector.tensor_copy(T.ysb[:], T.po[:, 0:QP]).then_inc(sem.sy, 1)
     g.sync.wait_ge(sem.sy, 1)
@@ -157,6 +186,7 @@ def rank_program(g, core, T, topo):
         _root_program(g, core, T, topo, direct, relay)
         return
 
+    left = 0
     if rank is not None and rank in direct:
         g.sync.dma_start(T.kv[:, 0:KP], T.k[:]).then_inc(sem.ld, 16)
         g.scalar.dma_start(T.kv[:, KP:2 * KP], T.v[:]).then_inc(sem.ld, 16)
@@ -165,33 +195,31 @@ def rank_program(g, core, T, topo):
         m = topo.mask(core, root)
         g.remote_dma(T.kv[:, 2 * rank * KP:(2 * rank + 2) * KP], T.kv[:, 0:2 * KP], sem["k%d" % rank], sem.sent,
                      pid, rid, m)
-        g.wait_ge(sem.sent, len(_bits(m)))
-        return
-
-    if rank is not None:
+        left += len(_bits(m))
+    elif rank is not None:
         g.sync.dma_start(T.st[0], T.k[:]).then_inc(sem.ld, 16)
         g.scalar.dma_start(T.st[1], T.v[:]).then_inc(sem.ld, 16)
         g.wait_ge(sem.ld, 32)
         xs = [relay[(rank, 0)], relay[(rank, 1)]]
-        eng = _bits(topo.mask(core, xs[0]) & topo.mask(core, xs[1]))
+        eng = _bits(topo.mask(core, xs[0][0]) & topo.mask(core, xs[1][0]))
         half = len(eng) // 2
-        step = half // 4
-        masks = [sum(eng[half::step]), sum(eng[0:half:step])]
+        masks = [_spread(eng[half:], E1), _spread(eng[:half], E1)]
         tr = []
         for piece in (0, 1):
-            rid, pid = topo.addr(xs[piece], core)
+            x, slot = xs[piece]
+            rid, pid = topo.addr(x, core)
             tr.append(RemoteDMATransfer(dst_ids=[DstId(rid=rid, pnc=pid)], dma_engine_mask=masks[piece],
-                                        remote_sem=sem.inn, src=T.st[piece], dst=T.rl[:]))
+                                        remote_sem=sem["inn%d" % slot], src=T.st[piece], dst=T.rl[slot]))
         g.remote_dma_fused(tr, local_sem=sem.sent)
-        g.wait_ge(sem.sent, len(_bits(masks[0])) + len(_bits(masks[1])))
-        return
+        left += 2 * E1
 
-    for (j, piece), x in relay.items():
-        if x != core:
-            continue
-        g.wait_ge(sem.inn, 4)
+    mine = sorted([(slot, j, piece) for (j, piece), (x, slot) in relay.items() if x == core])
+    for slot, j, piece in mine:
+        g.wait_ge(sem["inn%d" % slot], E1)
         rid, pid = topo.addr(root, core)
-        m = topo.mask(core, root)
+        m = _spread(_bits(topo.mask(core, root)), E2)
         a = (2 * j + piece) * KP
-        g.remote_dma(T.kv[:, a:a + KP], T.rl[:], sem["%s%d" % ("kv"[piece], j)], sem.sent, pid, rid, m)
-        g.wait_ge(sem.sent, len(_bits(m)))
+        g.remote_dma(T.kv[:, a:a + KP], T.rl[slot], sem["%s%d" % ("kv"[piece], j)], sem.sent, pid, rid, m)
+        left += E2
+    if left:
+        g.wait_ge(sem.sent, left)

from concourse.bass import DstId, RemoteDMATransfer
from concourse.mybir import AluOpType

N = 12
KP = 128
QP = 64
NG = 7
HOSTS = 4
E1 = 4
E2 = 8

SCRATCH = {
    "kv": ("sbuf", [128, N * 2 * KP], "bfloat16"),
    "qs": ("sbuf", [128, QP], "bfloat16"),
    "sb": ("sbuf", [128, N * QP], "bfloat16"),
    "zero": ("sbuf", [128, 2 * QP], "float32"),
    "ysb": ("sbuf", [128, QP], "bfloat16"),
    "st": ("dram", [2, 128, KP], "bfloat16"),
    "rl": ("dram", [2, 128, KP], "bfloat16"),
    "po": ("psum", [128, 512], "float32"),
}
for _b in range(NG):
    SCRATCH["ps%d" % _b] = ("psum", [128, 512], "float32")
SEMAPHORES = (["ld", "sent", "inn0", "inn1", "zs", "so", "sy", "st"]
              + ["s%d" % b for b in range(NG)] + ["r%d" % b for b in range(NG)]
              + ["k%d" % j for j in range(1, N)] + ["v%d" % j for j in range(1, N)])

_CACHE = {}


def _bits(m):
    return [1 << i for i in range(16) if (m >> i) & 1]


def _spread(eng, n):
    return sum(eng[::len(eng) // n])


def _plan(T, topo):
    if "plan" in _CACHE:
        return _CACHE["plan"]
    cores = list(T.cores)
    root = cores[T.root]
    by_chip = {}
    for c in range(HOSTS * topo.CORES_PER_HOST):
        by_chip.setdefault((topo.host(c), topo.chip(c)), []).append(c)

    def key(c):
        return (topo.host(c), topo.chip(c))

    def mate_key(c):
        for kk, cs in by_chip.items():
            if topo.mates(c, cs[0]):
                return kk

    def owners(kk):
        other = by_chip[mate_key(by_chip[kk][0])][0]
        return [x for x in by_chip[kk] if topo.may_write(x, other)]

    load = {}

    def give(x):
        load[x] = load.get(x, 0) + 1
        return (x, load[x] - 1)

    def fresh(pool, d):
        return give([x for x in pool if x not in cores and x not in load and topo.die(x) == d][0])

    def again(pool, d):
        return give([x for x in pool if load.get(x, 0) == 1 and topo.die(x) == d][0])

    direct = [j for j, s in enumerate(cores) if s != root and topo.may_write(s, root)]
    relay = {}
    over_mate = set()
    for j, s in enumerate(cores):
        if s == root or j in direct:
            continue
        my_rack = topo.rack(topo.host(s))
        root_rack = topo.rack(topo.host(root))
        d_own = topo.die(s)
        d_other = [d for d in (0, 1) if d != d_own][0]
        if [x for x in owners(key(s)) if topo.may_write(x, root)]:
            kk = key(s)
            if my_rack not in over_mate:
                over_mate.add(my_rack)
                kk = (topo.host(root) if my_rack == root_rack else topo.host(s), mate_key(root)[1])
            relay[(j, 0)] = fresh(owners(kk), d_own)
            relay[(j, 1)] = fresh(owners(kk), d_other)
        elif topo.chip(s) == topo.chip(root):
            via = [cores[d] for d in direct if topo.may_write(s, cores[d])]
            near = [x for x in via if topo.rack(topo.host(x)) == my_rack][0]
            far = [x for x in via if topo.rack(topo.host(x)) != my_rack][0]
            own = owners(key(near))
            relay[(j, 0)] = fresh([x for x in by_chip[key(near)] if x not in own], d_other)
            relay[(j, 1)] = give(far)
        else:
            kk = [k2 for k2 in by_chip if k2[1] == topo.chip(s) and topo.rack(k2[0]) == root_rack
                  and topo.may_write(s, by_chip[k2][0])][0]
            relay[(j, 0)] = again(owners(kk), d_own)
            relay[(j, 1)] = again(owners(kk), d_other)
    _CACHE["plan"] = (direct, relay)
    return _CACHE["plan"]


def _root_program(g, core, T, topo, direct, relay):
    sem = T.sem
    g.sync.dma_start(T.qs[:], T.q[:]).then_inc(sem.ld, 16)
    g.scalar.dma_start(T.kv[:, 0:KP], T.k[:]).then_inc(sem.ld, 16)
    g.sync.dma_start(T.kv[:, KP:2 * KP], T.v[:]).then_inc(sem.ld, 16)
    g.vector.memset(T.zero[:], 0.0).then_inc(sem.zs, 1)
    g.vector.wait_ge(sem.zs, 1)
    g.tensor.wait_ge(sem.ld, 48)

    cores = list(T.cores)

    def hops(j):
        if j == T.root:
            return 0
        if j in direct:
            return 1
        x = relay[(j, 0)][0]
        on_chip = (topo.host(x), topo.chip(x)) == (topo.host(cores[j]), topo.chip(cores[j]))
        return 2 if on_chip else 3

    groups = []
    place = 0
    for cl in range(4):
        js = [j for j in range(N) if hops(j) == cl]
        js.sort(key=lambda j: (relay[(j, 0)][1] if (j, 0) in relay else 0, j))
        for a in range(0, len(js), 2):
            groups.append((cl, js[a:a + 2], place))
            place += len(js[a:a + 2])
    total = [0]

    def landed(j, piece):
        if j == T.root or (piece == 1 and j in direct):
            return
        n = len(_bits(topo.mask(cores[j], core))) if j in direct else E2
        g.tensor.wait_ge(sem["%s%d" % ("kv"[piece], j)], n)

    def first(gi):
        _, js, at = groups[gi]
        ps = T["ps%d" % gi]
        for t, j in enumerate(js):
            landed(j, 0)
            g.tensor.matmul(ps[:, t * QP:(t + 1) * QP], T.kv[:, 2 * j * KP:(2 * j + 1) * KP], T.qs[:],
                            start=True, stop=True).then_inc(sem["s%d" % gi], 1)
        w = len(js) * QP
        g.vector.wait_ge(sem["s%d" % gi], len(js))
        g.vector.tensor_tensor(T.sb[:, at * QP:at * QP + w], ps[:, 0:w], T.zero[:, 0:w],
                               op=AluOpType.max).then_inc(sem["r%d" % gi], 1)

    def second(gi):
        _, js, at = groups[gi]
        g.tensor.wait_ge(sem["r%d" % gi], 1)
        for t, j in enumerate(js):
            landed(j, 1)
            total[0] += 1
            mm = g.tensor.matmul(T.po[:, 0:QP], T.kv[:, (2 * j + 1) * KP:(2 * j + 2) * KP],
                                 T.sb[:, (at + t) * QP:(at + t + 1) * QP], start=(total[0] == 1), stop=(total[0] == N))
            if total[0] == N:
                mm.then_inc(sem.so, 1)

    early = [gi for gi in range(len(groups)) if groups[gi][0] <= 1]
    late = [gi for gi in range(len(groups)) if groups[gi][0] > 1]
    for part in (early, late):
        for gi in part:
            first(gi)
        for gi in part:
            second(gi)
    g.vector.wait_ge(sem.so, 1)
    g.vector.tensor_copy(T.ysb[:], T.po[:, 0:QP]).then_inc(sem.sy, 1)
    g.sync.wait_ge(sem.sy, 1)
    g.sync.dma_start(T.y[:], T.ysb[:]).then_inc(sem.st, 16)
    g.sync.wait_ge(sem.st, 16)


def rank_program(g, core, T, topo):
    direct, relay = _plan(T, topo)
    cores = list(T.cores)
    root = cores[T.root]
    sem = T.sem
    rank = T.rank_of(core)

    if core == root:
        _root_program(g, core, T, topo, direct, relay)
        return

    left = 0
    if rank is not None and rank in direct:
        g.sync.dma_start(T.kv[:, 0:KP], T.k[:]).then_inc(sem.ld, 16)
        g.scalar.dma_start(T.kv[:, KP:2 * KP], T.v[:]).then_inc(sem.ld, 16)
        g.wait_ge(sem.ld, 32)
        rid, pid = topo.addr(root, core)
        m = topo.mask(core, root)
        g.remote_dma(T.kv[:, 2 * rank * KP:(2 * rank + 2) * KP], T.kv[:, 0:2 * KP], sem["k%d" % rank], sem.sent,
                     pid, rid, m)
        left += len(_bits(m))
    elif rank is not None:
        g.sync.dma_start(T.st[0], T.k[:]).then_inc(sem.ld, 16)
        g.scalar.dma_start(T.st[1], T.v[:]).then_inc(sem.ld, 16)
        g.wait_ge(sem.ld, 32)
        xs = [relay[(rank, 0)], relay[(rank, 1)]]
        eng = _bits(topo.mask(core, xs[0][0]) & topo.mask(core, xs[1][0]))
        half = len(eng) // 2
        masks = [_spread(eng[half:], E1), _spread(eng[:half], E1)]
        tr = []
        for piece in (0, 1):
            x, slot = xs[piece]
            rid, pid = topo.addr(x, core)
            tr.append(RemoteDMATransfer(dst_ids=[DstId(rid=rid, pnc=pid)], dma_engine_mask=masks[piece],
                                        remote_sem=sem["inn%d" % slot], src=T.st[piece], dst=T.rl[slot]))
        g.remote_dma_fused(tr, local_sem=sem.sent)
        left += 2 * E1

    mine = sorted([(slot, j, piece) for (j, piece), (x, slot) in relay.items() if x == core])
    for slot, j, piece in mine:
        g.wait_ge(sem["inn%d" % slot], E1)
        rid, pid = topo.addr(root, core)
        m = _spread(_bits(topo.mask(core, root)), E2)
        a = (2 * j + piece) * KP
        g.remote_dma(T.kv[:, a:a + KP], T.rl[slot], sem["%s%d" % ("kv"[piece], j)], sem.sent, pid, rid, m)
        left += E2
    if left:
        g.wait_ge(sem.sent, left)
